import numpy as np
import ml_dtypes


def mxq(x, axis, fmt="e4m3"):
    dtype, down = {"e4m3": (ml_dtypes.float8_e4m3fn, 7), "e5m2": (ml_dtypes.float8_e5m2, 14)}[fmt]
    v = np.moveaxis(np.asarray(x, np.float32).astype(ml_dtypes.bfloat16).astype(np.float64), axis, -1)
    blocks = v.reshape(v.shape[:-1] + (-1, 32))
    amax = np.abs(blocks).max(-1, keepdims=True)
    byte = np.maximum(np.where(amax > 0, np.frexp(amax)[1] - 1 + 127, 0) - down, 1)
    scale = np.exp2(byte - 127.0)
    codes = (blocks / scale).astype(np.float32).astype(dtype).astype(np.float64)
    return np.moveaxis((codes * scale).reshape(v.shape), -1, axis)


WIDE = False


def mx_kscale(k):
    if not WIDE:
        return np.ones(k)
    levels = np.array([30, -30])
    if k % 512:
        return np.exp2(np.random.permutation(np.resize(levels, k // 32))).repeat(32)
    a = np.empty((k // 512, 16))
    for p in range(k // 512):
        a[p, :8] = np.random.permutation(np.resize(levels, 8))
        for g in range(8):
            far = levels[np.abs(levels - a[p, g]) >= 10]
            a[p, g + 8] = far[np.random.randint(len(far))]
    return np.exp2(a.ravel()).repeat(32)


def f64(x):
    return np.asarray(x).astype(np.float64)


def striped(idx):
    return np.tile(np.asarray(idx).reshape(-1, 16).T, (8, 1)).astype(np.uint16)


def unstriped(offs):
    return offs[:16].T.reshape(-1).astype(np.int64)


def striped8(idx):
    return np.asarray(idx).reshape(8, -1, 16).transpose(0, 2, 1).reshape(128, -1).astype(np.uint16)


def unstriped8(offs):
    return offs.reshape(8, 16, -1).transpose(0, 2, 1).reshape(8, -1).astype(np.int64)


def pick8(x, idx, run):
    r = np.arange(len(x))
    return x[r[:, None], idx[r % (8 * run) // run]]


def bf(x):
    return np.asarray(x, np.float32).astype(ml_dtypes.bfloat16)


def planes(Y):
    r, m = Y.shape
    b = f64(bf(Y)).reshape(r // 32, 32, m)
    amax = np.abs(b).max(1)
    byte = np.clip(np.where(amax > 0, np.frexp(amax)[1] - 1 + 127 - 7, 1), 1, 254)
    codes = (b * np.exp2(127.0 - byte)[:, None, :]).reshape(r, m).astype(np.float32).astype(ml_dtypes.float8_e4m3fn).view(np.uint8)
    words = codes.reshape(r // 512, 128, 4, m).transpose(0, 1, 3, 2)
    return np.ascontiguousarray(words), np.ascontiguousarray(byte.astype(np.uint8).reshape(r // 512, 16, m))


K, J, N, T, V = 512, 512, 256, 1024, 1024


def setup_inputs():
    n = np.random.standard_normal
    idx = np.stack([np.random.permutation(T)[:J] for _ in range(8)])
    idx2 = np.random.permutation(V)[:J]
    idx3 = np.random.permutation(V)[:J]
    fj = mx_kscale(J)
    return {
        "xf": (n((K, T))).astype(np.float32),
        "ra": (np.random.uniform(0.5, 1.5, (1, J)) * fj).astype(np.float32),
        "gt": (n((N, V)) * np.exp(0.5 * n((1, V)))).astype(np.float32),
        "rb": (np.random.uniform(0.5, 1.5, (1, J)) / fj).astype(np.float32),
        "mom": (1.0 * n((K, N))).astype(np.float32),
        "old": (1.0 * n((K, N))).astype(np.float32),
        "offs": striped8(idx),
        "offs2": striped(idx2),
        "offs3": striped(idx3),
    }


def reference(xf, ra, gt, rb, mom, old, offs, offs2, offs3):
    idx = unstriped8(offs)
    idx2 = unstriped(offs2)
    idx3 = unstriped(offs3)
    us = pick8(f64(xf), idx, 64) * f64(ra)
    uj = us.T
    gs = (f64(gt)[:, idx2] - 0.7 * f64(gt)[:, idx3]) * f64(rb)
    gj = gs.T
    ujq = mxq(uj, 0, "e5m2")
    gjq = mxq(gj, 0, "e5m2")
    w = ujq.T @ gjq
    u2 = 0.04 * w + 0.6 * f64(mom)
    y = f64(old) * 0.5 - u2 / (1.0 + np.abs(u2))
    words, scales = planes(y)
    return y, words, scales

@@ -1,0 +1,182 @@
+from contextlib import ExitStack
+
+import concourse.mybir as mybir
+from concourse.masks import make_identity
+
+K, J, N, T, V = 512, 512, 256, 1024, 1024
+FLOPS = 2 * K * J * N
+
+F32 = mybir.dt.float32
+BF16 = mybir.dt.bfloat16
+I32 = mybir.dt.int32
+U32 = mybir.dt.uint32
+U16 = mybir.dt.uint16
+U8 = mybir.dt.uint8
+E5M2X4 = mybir.dt.float8_e5m2_x4
+E4M3X4 = mybir.dt.float8_e4m3fn_x4
+ALU = mybir.AluOpType
+ACT = mybir.ActivationFunctionType
+
+P = 128
+PACK = 4
+LIST_COLS = J // 16
+
+
+def tile_list_moment_headpicks_differences_momentum_pl_kernel(
+    tc, xf, ra, gt, rb, mom, old, offs, offs2, offs3, out_0, out_1, out_2
+):
+    nc = tc.nc
+    with ExitStack() as ctx:
+        keep = ctx.enter_context(tc.tile_pool(name="keep", bufs=1))
+        turn_ps = ctx.enter_context(tc.psum_pool(name="turn_ps", bufs=4))
+        acc_ps = ctx.enter_context(tc.psum_pool(name="acc_ps", bufs=1))
+
+        list_x = keep.tile([P, LIST_COLS], U16, name="list_x")
+        list_a = keep.tile([P, LIST_COLS], U16, name="list_a")
+        list_b = keep.tile([P, LIST_COLS], U16, name="list_b")
+        g_rows = [keep.tile([P, V], F32, name="g_rows%d" % h) for h in range(2)]
+        x_rows = [keep.tile([P, T], F32, name="x_rows%d" % i) for i in range(PACK)]
+        ra_col = keep.tile([P, PACK], F32, name="ra_col")
+        rb_col = keep.tile([P, PACK], F32, name="rb_col")
+        mom_sb = [keep.tile([P, 2 * N], F32, name="mom_sb%d" % h) for h in range(2)]
+        old_sb = [keep.tile([P, 2 * N], F32, name="old_sb%d" % h) for h in range(2)]
+        ident = keep.tile([P, P], F32, name="ident")
+
+        x_planes = xf.rearrange("(p i) t -> p i t", i=PACK)
+        nc.scalar.dma_start(rb_col[:], rb.rearrange("o (q t) -> (o q) t", t=PACK))
+        nc.scalar.dma_start(ra_col[:], ra.rearrange("o (q t) -> (o q) t", t=PACK))
+        mom_hbm = mom.rearrange("(p i) n -> p (i n)", i=PACK)
+        old_hbm = old.rearrange("(p i) n -> p (i n)", i=PACK)
+        nc.sync.dma_start(g_rows[0][:], gt[0:P, :])
+        nc.sync.dma_start(list_b[:], offs3)
+        nc.sync.dma_start(list_a[:], offs2)
+        nc.sync.dma_start(g_rows[1][:], gt[P : 2 * P, :])
+        nc.sync.dma_start(list_x[:], offs)
+        nc.sync.dma_start(x_rows[0][:], x_planes[:, 0, :])
+        nc.sync.dma_start(x_rows[1][:], x_planes[:, 1, :])
+        nc.sync.dma_start(x_rows[2][:], x_planes[:, 2, :])
+        nc.sync.dma_start(x_rows[3][:], x_planes[:, 3, :])
+        nc.sync.dma_start(mom_sb[0][:], mom_hbm[:, 0 * 2 * N : 1 * 2 * N])
+        nc.sync.dma_start(mom_sb[1][:], mom_hbm[:, 1 * 2 * N : 2 * 2 * N])
+        nc.sync.dma_start(old_sb[0][:], old_hbm[:, 0 * 2 * N : 1 * 2 * N])
+        nc.sync.dma_start(old_sb[1][:], old_hbm[:, 1 * 2 * N : 2 * 2 * N])
+
+        make_identity(nc, ident[:])
+
+        def halves(n):
+            w = LIST_COLS // n
+            return [(slice(c * w, (c + 1) * w), slice(16 * c * w, 16 * (c + 1) * w)) for c in range(n)]
+
+        def turn_wide(picked, col, grouped):
+            turned = turn_ps.tile([P, PACK, P], F32, name="turned")
+            by_byte = picked[:].rearrange("p (q t) -> p t q", t=PACK)
+            for t in range(PACK):
+                nc.tensor.transpose(turned[:, t, :], by_byte[:, t, :], ident[:])
+            nc.vector.tensor_tensor(
+                grouped.rearrange("q (r t) -> q r t", t=PACK),
+                turned[:].rearrange("q t r -> q r t"),
+                col[:].unsqueeze(1).to_broadcast([P, P, PACK]),
+                ALU.mult,
+            )
+
+        g_grouped = keep.tile([P, N * PACK], BF16, name="g_grouped", align_bytes=64)
+        g_codes = keep.tile([P, N], U32, name="g_codes", align_bytes=64)
+        g_scales = keep.tile([P, N], U8, name="g_scales", align_bytes=64)
+
+        def pick_g(h, pieces):
+            minus_b = keep.tile([P, J], F32, name="minus_b%d" % h)
+            diff = keep.tile([P, J], F32, name="diff%d" % h)
+            for cols, slots in halves(pieces):
+                nc.scalar.activation(minus_b[:, slots], g_rows[h][:].indirect(list_b[:, cols]), ACT.Copy, scale=-0.7)
+                nc.vector.tensor_tensor(diff[:, slots], g_rows[h][:].indirect(list_a[:, cols]), minus_b[:, slots], ALU.add)
+            return diff
+
+        def pick_x(i, engines):
+            picked = keep.tile([P, J], F32, name="x_picked%d" % i)
+            for engine, (cols, slots) in zip(engines, halves(len(engines))):
+                window = x_rows[i][:].indirect(list_x[:, cols])
+                if engine == "S":
+                    nc.scalar.activation(picked[:, slots], window, ACT.Copy)
+                else:
+                    nc.vector.tensor_copy(picked[:, slots], window)
+            return picked
+
+        accs = [acc_ps.tile([P, N], F32, name="acc%d" % i) for i in range(PACK)]
+
+        def moment(i, values):
+            grouped = keep.tile([P, P * PACK], BF16, name="x_grouped%d" % i, align_bytes=64)
+            codes = keep.tile([P, P], U32, name="x_codes%d" % i, align_bytes=64)
+            scales = keep.tile([P, P], U8, name="x_scales%d" % i, align_bytes=64)
+            turn_wide(values, ra_col, grouped[:])
+            nc.vector.quantize_mx(out=codes[:].bitcast(E5M2X4), scales=scales[:], in_=grouped[:])
+            nc.tensor.matmul_mx(
+                out=accs[i][:],
+                lhsT=codes[:].bitcast(E5M2X4),
+                lhsT_scale=scales[:],
+                rhs=g_codes[:].bitcast(E5M2X4),
+                rhs_scale=g_scales[:],
+                start=True,
+                stop=True,
+            )
+
+        y_sb = keep.tile([P, PACK * N], F32, name="y_sb")
+        y_hbm = out_0.rearrange("(p i) n -> p (i n)", i=PACK)
+
+        def step(i, lo, hi):
+            name = "%d_%d" % (i, lo)
+            width = hi - lo
+            given = slice((i % 2) * N + lo, (i % 2) * N + hi)
+            v = keep.tile([P, width], F32, name="v" + name)
+            size = keep.tile([P, width], F32, name="size" + name)
+            root = keep.tile([P, width], F32, name="root" + name)
+            inverse = keep.tile([P, width], F32, name="inverse" + name)
+            soft = keep.tile([P, width], F32, name="soft" + name)
+            nc.vector.scalar_tensor_tensor(v[:], accs[i][:, lo:hi], 0.04 / 0.6, mom_sb[i // 2][:, given], ALU.mult, ALU.add)
+            nc.scalar.activation(size[:], v[:], ACT.Abs, scale=0.6)
+            nc.scalar.activation(root[:], size[:], ACT.Abs_reciprocal_sqrt, bias=1.0)
+            nc.scalar.activation(inverse[:], root[:], ACT.Square)
+            nc.vector.scalar_tensor_tensor(soft[:], v[:], 0.6, inverse[:], ALU.mult, ALU.mult)
+            nc.vector.scalar_tensor_tensor(
+                y_sb[:, i * N + lo : i * N + hi], old_sb[i // 2][:, given], 0.5, soft[:], ALU.mult, ALU.subtract
+            )
+
+        g0 = pick_g(0, 2)
+        g1 = pick_g(1, 2)
+        turn_wide(g0, rb_col, g_grouped[:, 0 * P * PACK : 1 * P * PACK])
+        x0 = pick_x(0, "S")
+        turn_wide(g1, rb_col, g_grouped[:, 1 * P * PACK : 2 * P * PACK])
+        x1 = pick_x(1, "S")
+        nc.vector.quantize_mx(out=g_codes[:].bitcast(E5M2X4), scales=g_scales[:], in_=g_grouped[:])
+        x2 = pick_x(2, "S")
+        moment(0, x0)
+        x3 = pick_x(3, "S")
+        moment(1, x1)
+        moment(2, x2)
+        moment(3, x3)
+        step(0, 0, N)
+        nc.sync.dma_start(y_hbm[:, 0 * N : 1 * N], y_sb[:, 0 * N : 1 * N])
+        step(1, 0, N)
+        nc.sync.dma_start(y_hbm[:, 1 * N : 2 * N], y_sb[:, 1 * N : 2 * N])
+        step(2, 0, N)
+        nc.sync.dma_start(y_hbm[:, 2 * N : 3 * N], y_sb[:, 2 * N : 3 * N])
+        step(3, 0, N // 2)
+        step(3, N // 2, N)
+        nc.sync.dma_start(y_hbm[:, 3 * N : 4 * N], y_sb[:, 3 * N : 4 * N])
+
+        y_codes = keep.tile([P, N], U32, name="y_codes", align_bytes=64)
+        y_scales = keep.tile([P, N], U8, name="y_scales", align_bytes=64)
+        y_planes = y_sb[:].rearrange("p (i n) -> p i n", i=PACK)
+        codes_hbm = out_1[0].rearrange("l c r -> l (c r)").bitcast(I32)
+        half = N // 2
+        y_grouped = [keep.tile([P, half * PACK], BF16, name="y_grouped%d" % c, align_bytes=64) for c in range(2)]
+        for c, copy in enumerate((nc.vector.tensor_copy, nc.vector.tensor_copy)):
+            cols = slice(c * half, (c + 1) * half)
+            copy(y_grouped[c][:].rearrange("p (n i) -> p n i", i=PACK), y_planes[:, :, cols].rearrange("p i n -> p n i"))
+        for c in range(2):
+            cols = slice(c * half, (c + 1) * half)
+            nc.vector.quantize_mx(out=y_codes[:, cols].bitcast(E4M3X4), scales=y_scales[:, cols], in_=y_grouped[c][:])
+            nc.sync.dma_start(codes_hbm[:, cols], y_codes[:, cols].bitcast(I32))
+        scales_hbm = out_2[0].bitcast(I32)
+        for quad in range(4):
+            queue = nc.sync if quad < 2 else nc.scalar
+            queue.dma_start(scales_hbm[4 * quad : 4 * quad + 4, :], y_scales[32 * quad : 32 * quad + 4, :].bitcast(I32))

@@ -61,6 +61,10 @@ def tile_list_moment_headpicks_differences_momentum_pl_kernel(
         nc.sync.dma_start(old_sb[0][:], old_hbm[:, 0 * 2 * N : 1 * 2 * N])
         nc.sync.dma_start(old_sb[1][:], old_hbm[:, 1 * 2 * N : 2 * 2 * N])
 
+        warm_in = keep.tile([P, 1], F32, name="warm_in")
+        warm_out = keep.tile([P, 1], F32, name="warm_out")
+        nc.vector.memset(warm_in[:], 1.0)
+        nc.scalar.activation(warm_out[:], warm_in[:], ACT.Abs_reciprocal_sqrt, bias=1.0)
         make_identity(nc, ident[:])
 
         def halves(n):

@@ -28,7 +28,8 @@ def tile_list_moment_headpicks_differences_momentum_pl_kernel(
     nc = tc.nc
     with ExitStack() as ctx:
         keep = ctx.enter_context(tc.tile_pool(name="keep", bufs=1))
-        turn_ps = ctx.enter_context(tc.psum_pool(name="turn_ps", bufs=4))
+        spread_ps = ctx.enter_context(tc.psum_pool(name="spread_ps", bufs=1))
+        turn_ps = ctx.enter_context(tc.psum_pool(name="turn_ps", bufs=2))
         acc_ps = ctx.enter_context(tc.psum_pool(name="acc_ps", bufs=1))
 
         list_x = keep.tile([P, LIST_COLS], U16, name="list_x")
@@ -55,10 +56,10 @@ def tile_list_moment_headpicks_differences_momentum_pl_kernel(
         nc.sync.dma_start(x_rows[0][:], x_planes[:, 0, :])
         nc.sync.dma_start(x_rows[1][:], x_planes[:, 1, :])
         nc.sync.dma_start(x_rows[2][:], x_planes[:, 2, :])
-        nc.sync.dma_start(x_rows[3][:], x_planes[:, 3, :])
         nc.sync.dma_start(mom_sb[0][:], mom_hbm[:, 0 * 2 * N : 1 * 2 * N])
-        nc.sync.dma_start(mom_sb[1][:], mom_hbm[:, 1 * 2 * N : 2 * 2 * N])
+        nc.sync.dma_start(x_rows[3][:], x_planes[:, 3, :])
         nc.sync.dma_start(old_sb[0][:], old_hbm[:, 0 * 2 * N : 1 * 2 * N])
+        nc.sync.dma_start(mom_sb[1][:], mom_hbm[:, 1 * 2 * N : 2 * 2 * N])
         nc.sync.dma_start(old_sb[1][:], old_hbm[:, 1 * 2 * N : 2 * 2 * N])
 
         warm_in = keep.tile([P, 1], F32, name="warm_in")
@@ -66,10 +67,34 @@ def tile_list_moment_headpicks_differences_momentum_pl_kernel(
         nc.vector.memset(warm_in[:], 1.0)
         nc.scalar.activation(warm_out[:], warm_in[:], ACT.Abs_reciprocal_sqrt, bias=1.0)
         make_identity(nc, ident[:])
+        rb_spread = spread_ps.tile([P, PACK, P], F32, name="rb_spread")
+        ra_spread = spread_ps.tile([P, PACK, P], F32, name="ra_spread")
+        for col, spread in ((rb_col, rb_spread), (ra_col, ra_spread),):
+            for t in range(PACK):
+                nc.tensor.transpose(spread[:, t, :], col[:, t : t + 1].to_broadcast([P, P]), ident[:])
 
         def halves(n):
             w = LIST_COLS // n
             return [(slice(c * w, (c + 1) * w), slice(16 * c * w, 16 * (c + 1) * w)) for c in range(n)]
+
+        def by_pairs(values):
+            return values.rearrange("p (q u e) -> p u q e", u=2, e=2)
+
+        def weigh_and_round(name, picked, spread):
+            pairs = keep.tile([P, 2, P, 2], BF16, name=name)
+            nc.vector.tensor_tensor(
+                pairs[:], by_pairs(picked[:]), spread[:].rearrange("p (u e) q -> p u q e", e=2), ALU.mult
+            )
+            return pairs
+
+        def turn(pairs, grouped, copy):
+            words = pairs[:].rearrange("p u q e -> p (u q e)").bitcast(F32)
+            turned = turn_ps.tile([P, 2, P], F32, name="turned")
+            for u in range(2):
+                nc.tensor.transpose(turned[:, u, :], words[:, u * P : (u + 1) * P], ident[:])
+            copy(
+                grouped.bitcast(F32).rearrange("q (r u) -> q r u", u=2), turned[:].rearrange("q u r -> q r u")
+            )
 
         def turn_wide(picked, col, grouped):
             turned = turn_ps.tile([P, PACK, P], F32, name="turned")
@@ -107,11 +132,14 @@ def tile_list_moment_headpicks_differences_momentum_pl_kernel(
 
         accs = [acc_ps.tile([P, N], F32, name="acc%d" % i) for i in range(PACK)]
 
-        def moment(i, values):
+        def moment(i, values, wide, copy):
             grouped = keep.tile([P, P * PACK], BF16, name="x_grouped%d" % i, align_bytes=64)
             codes = keep.tile([P, P], U32, name="x_codes%d" % i, align_bytes=64)
             scales = keep.tile([P, P], U8, name="x_scales%d" % i, align_bytes=64)
-            turn_wide(values, ra_col, grouped[:])
+            if wide:
+                turn_wide(values, ra_col, grouped[:])
+            else:
+                turn(values, grouped[:], copy)
             nc.vector.quantize_mx(out=codes[:].bitcast(E5M2X4), scales=scales[:], in_=grouped[:])
             nc.tensor.matmul_mx(
                 out=accs[i][:],
@@ -126,7 +154,7 @@ def tile_list_moment_headpicks_differences_momentum_pl_kernel(
         y_sb = keep.tile([P, PACK * N], F32, name="y_sb")
         y_hbm = out_0.rearrange("(p i) n -> p (i n)", i=PACK)
 
-        def step(i, lo, hi):
+        def step(i, lo, hi, abs_on_vector):
             name = "%d_%d" % (i, lo)
             width = hi - lo
             given = slice((i % 2) * N + lo, (i % 2) * N + hi)
@@ -136,8 +164,11 @@ def tile_list_moment_headpicks_differences_momentum_pl_kernel(
             inverse = keep.tile([P, width], F32, name="inverse" + name)
             soft = keep.tile([P, width], F32, name="soft" + name)
             nc.vector.scalar_tensor_tensor(v[:], accs[i][:, lo:hi], 0.04 / 0.6, mom_sb[i // 2][:, given], ALU.mult, ALU.add)
-            nc.scalar.activation(size[:], v[:], ACT.Abs, scale=0.6)
-            nc.scalar.activation(root[:], size[:], ACT.Abs_reciprocal_sqrt, bias=1.0)
+            if abs_on_vector:
+                nc.vector.scalar_tensor_tensor(size[:], v[:], -1.0, v[:], ALU.mult, ALU.max)
+            else:
+                nc.scalar.activation(size[:], v[:], ACT.Abs)
+            nc.scalar.activation(root[:], size[:], ACT.Abs_reciprocal_sqrt, bias=1.0, scale=0.6)
             nc.scalar.activation(inverse[:], root[:], ACT.Square)
             nc.vector.scalar_tensor_tensor(soft[:], v[:], 0.6, inverse[:], ALU.mult, ALU.mult)
             nc.vector.scalar_tensor_tensor(
@@ -145,26 +176,33 @@ def tile_list_moment_headpicks_differences_momentum_pl_kernel(
             )
 
         g0 = pick_g(0, 2)
+        g0 = weigh_and_round("g_pairs0", g0, rb_spread)
         g1 = pick_g(1, 2)
-        turn_wide(g0, rb_col, g_grouped[:, 0 * P * PACK : 1 * P * PACK])
+        g1 = weigh_and_round("g_pairs1", g1, rb_spread)
+        turn(g0, g_grouped[:, 0 * P * PACK : 1 * P * PACK], nc.vector.tensor_copy)
         x0 = pick_x(0, "S")
-        turn_wide(g1, rb_col, g_grouped[:, 1 * P * PACK : 2 * P * PACK])
+        x0 = weigh_and_round("x_pairs0", x0, ra_spread)
+        turn(g1, g_grouped[:, 1 * P * PACK : 2 * P * PACK], nc.vector.tensor_copy)
         x1 = pick_x(1, "S")
+        x1 = weigh_and_round("x_pairs1", x1, ra_spread)
         nc.vector.quantize_mx(out=g_codes[:].bitcast(E5M2X4), scales=g_scales[:], in_=g_grouped[:])
         x2 = pick_x(2, "S")
-        moment(0, x0)
+        x2 = weigh_and_round("x_pairs2", x2, ra_spread)
+        moment(0, x0, False, nc.scalar.copy)
         x3 = pick_x(3, "S")
-        moment(1, x1)
-        moment(2, x2)
-        moment(3, x3)
-        step(0, 0, N)
+        x3 = weigh_and_round("x_pairs3", x3, ra_spread)
+        moment(1, x1, False, nc.scalar.copy)
+        moment(2, x2, False, nc.scalar.copy)
+        moment(3, x3, False, nc.scalar.copy)
+        step(0, 0, N // 2, True)
+        step(0, N // 2, N, True)
         nc.sync.dma_start(y_hbm[:, 0 * N : 1 * N], y_sb[:, 0 * N : 1 * N])
-        step(1, 0, N)
+        step(1, 0, N, True)
         nc.sync.dma_start(y_hbm[:, 1 * N : 2 * N], y_sb[:, 1 * N : 2 * N])
-        step(2, 0, N)
+        step(2, 0, N, False)
         nc.sync.dma_start(y_hbm[:, 2 * N : 3 * N], y_sb[:, 2 * N : 3 * N])
-        step(3, 0, N // 2)
-        step(3, N // 2, N)
+        step(3, 0, N // 2, False)
+        step(3, N // 2, N, False)
         nc.sync.dma_start(y_hbm[:, 3 * N : 4 * N], y_sb[:, 3 * N : 4 * N])
 
         y_codes = keep.tile([P, N], U32, name="y_codes", align_bytes=64)

from contextlib import ExitStack

import concourse.mybir as mybir
from concourse.masks import make_identity

K, J, N, T, V = 512, 512, 256, 1024, 1024
FLOPS = 2 * K * J * N

F32 = mybir.dt.float32
BF16 = mybir.dt.bfloat16
I32 = mybir.dt.int32
U32 = mybir.dt.uint32
U16 = mybir.dt.uint16
U8 = mybir.dt.uint8
E5M2X4 = mybir.dt.float8_e5m2_x4
E4M3X4 = mybir.dt.float8_e4m3fn_x4
ALU = mybir.AluOpType
ACT = mybir.ActivationFunctionType

P = 128
PACK = 4
LIST_COLS = J // 16


def tile_list_moment_headpicks_differences_momentum_pl_kernel(
    tc, xf, ra, gt, rb, mom, old, offs, offs2, offs3, out_0, out_1, out_2
):
    nc = tc.nc
    with ExitStack() as ctx:
        keep = ctx.enter_context(tc.tile_pool(name="keep", bufs=1))
        spread_ps = ctx.enter_context(tc.psum_pool(name="spread_ps", bufs=1))
        turn_ps = ctx.enter_context(tc.psum_pool(name="turn_ps", bufs=2))
        acc_ps = ctx.enter_context(tc.psum_pool(name="acc_ps", bufs=1))

        list_x = keep.tile([P, LIST_COLS], U16, name="list_x")
        list_a = keep.tile([P, LIST_COLS], U16, name="list_a")
        list_b = keep.tile([P, LIST_COLS], U16, name="list_b")
        g_rows = [keep.tile([P, V], F32, name="g_rows%d" % h) for h in range(2)]
        x_rows = [keep.tile([P, T], F32, name="x_rows%d" % i) for i in range(PACK)]
        ra_col = keep.tile([P, PACK], F32, name="ra_col")
        rb_col = keep.tile([P, PACK], F32, name="rb_col")
        mom_sb = [keep.tile([P, 2 * N], F32, name="mom_sb%d" % h) for h in range(2)]
        old_sb = [keep.tile([P, 2 * N], F32, name="old_sb%d" % h) for h in range(2)]
        ident = keep.tile([P, P], F32, name="ident")

        x_planes = xf.rearrange("(p i) t -> p i t", i=PACK)
        nc.scalar.dma_start(rb_col[:], rb.rearrange("o (q t) -> (o q) t", t=PACK))
        nc.scalar.dma_start(ra_col[:], ra.rearrange("o (q t) -> (o q) t", t=PACK))
        mom_hbm = mom.rearrange("(p i) n -> p (i n)", i=PACK)
        old_hbm = old.rearrange("(p i) n -> p (i n)", i=PACK)
        nc.sync.dma_start(g_rows[0][:], gt[0:P, :])
        nc.sync.dma_start(list_b[:], offs3)
        nc.sync.dma_start(list_a[:], offs2)
        nc.sync.dma_start(g_rows[1][:], gt[P : 2 * P, :])
        nc.sync.dma_start(list_x[:], offs)
        nc.sync.dma_start(x_rows[0][:], x_planes[:, 0, :])
        nc.sync.dma_start(x_rows[1][:], x_planes[:, 1, :])
        nc.sync.dma_start(x_rows[2][:], x_planes[:, 2, :])
        nc.sync.dma_start(mom_sb[0][:], mom_hbm[:, 0 * 2 * N : 1 * 2 * N])
        nc.sync.dma_start(x_rows[3][:], x_planes[:, 3, :])
        nc.sync.dma_start(old_sb[0][:], old_hbm[:, 0 * 2 * N : 1 * 2 * N])
        nc.sync.dma_start(mom_sb[1][:], mom_hbm[:, 1 * 2 * N : 2 * 2 * N])
        nc.sync.dma_start(old_sb[1][:], old_hbm[:, 1 * 2 * N : 2 * 2 * N])

        warm_in = keep.tile([P, 1], F32, name="warm_in")
        warm_out = keep.tile([P, 1], F32, name="warm_out")
        nc.vector.memset(warm_in[:], 1.0)
        nc.scalar.activation(warm_out[:], warm_in[:], ACT.Abs_reciprocal_sqrt, bias=1.0)
        make_identity(nc, ident[:])
        rb_spread = spread_ps.tile([P, PACK, P], F32, name="rb_spread")
        ra_spread = spread_ps.tile([P, PACK, P], F32, name="ra_spread")
        for col, spread in ((rb_col, rb_spread), (ra_col, ra_spread),):
            for t in range(PACK):
                nc.tensor.transpose(spread[:, t, :], col[:, t : t + 1].to_broadcast([P, P]), ident[:])

        def halves(n):
            w = LIST_COLS // n
            return [(slice(c * w, (c + 1) * w), slice(16 * c * w, 16 * (c + 1) * w)) for c in range(n)]

        def by_pairs(values):
            return values.rearrange("p (q u e) -> p u q e", u=2, e=2)

        def weigh_and_round(name, picked, spread):
            pairs = keep.tile([P, 2, P, 2], BF16, name=name)
            nc.vector.tensor_tensor(
                pairs[:], by_pairs(picked[:]), spread[:].rearrange("p (u e) q -> p u q e", e=2), ALU.mult
            )
            return pairs

        def turn(pairs, grouped, copy):
            words = pairs[:].rearrange("p u q e -> p (u q e)").bitcast(F32)
            turned = turn_ps.tile([P, 2, P], F32, name="turned")
            for u in range(2):
                nc.tensor.transpose(turned[:, u, :], words[:, u * P : (u + 1) * P], ident[:])
            copy(
                grouped.bitcast(F32).rearrange("q (r u) -> q r u", u=2), turned[:].rearrange("q u r -> q r u")
            )

        def turn_wide(picked, col, grouped):
            turned = turn_ps.tile([P, PACK, P], F32, name="turned")
            by_byte = picked[:].rearrange("p (q t) -> p t q", t=PACK)
            for t in range(PACK):
                nc.tensor.transpose(turned[:, t, :], by_byte[:, t, :], ident[:])
            nc.vector.tensor_tensor(
                grouped.rearrange("q (r t) -> q r t", t=PACK),
                turned[:].rearrange("q t r -> q r t"),
                col[:].unsqueeze(1).to_broadcast([P, P, PACK]),
                ALU.mult,
            )

        g_grouped = keep.tile([P, N * PACK], BF16, name="g_grouped", align_bytes=64)
        g_codes = keep.tile([P, N], U32, name="g_codes", align_bytes=64)
        g_scales = keep.tile([P, N], U8, name="g_scales", align_bytes=64)

        def pick_g(h, pieces):
            minus_b = keep.tile([P, J], F32, name="minus_b%d" % h)
            diff = keep.tile([P, J], F32, name="diff%d" % h)
            for cols, slots in halves(pieces):
                nc.scalar.activation(minus_b[:, slots], g_rows[h][:].indirect(list_b[:, cols]), ACT.Copy, scale=-0.7)
                nc.vector.tensor_tensor(diff[:, slots], g_rows[h][:].indirect(list_a[:, cols]), minus_b[:, slots], ALU.add)
            return diff

        def pick_x(i, engines):
            picked = keep.tile([P, J], F32, name="x_picked%d" % i)
            for engine, (cols, slots) in zip(engines, halves(len(engines))):
                window = x_rows[i][:].indirect(list_x[:, cols])
                if engine == "S":
                    nc.scalar.activation(picked[:, slots], window, ACT.Copy)
                else:
                    nc.vector.tensor_copy(picked[:, slots], window)
            return picked

        accs = [acc_ps.tile([P, N], F32, name="acc%d" % i) for i in range(PACK)]

        def moment(i, values, wide, copy):
            grouped = keep.tile([P, P * PACK], BF16, name="x_grouped%d" % i, align_bytes=64)
            codes = keep.tile([P, P], U32, name="x_codes%d" % i, align_bytes=64)
            scales = keep.tile([P, P], U8, name="x_scales%d" % i, align_bytes=64)
            if wide:
                turn_wide(values, ra_col, grouped[:])
            else:
                turn(values, grouped[:], copy)
            nc.vector.quantize_mx(out=codes[:].bitcast(E5M2X4), scales=scales[:], in_=grouped[:])
            nc.tensor.matmul_mx(
                out=accs[i][:],
                lhsT=codes[:].bitcast(E5M2X4),
                lhsT_scale=scales[:],
                rhs=g_codes[:].bitcast(E5M2X4),
                rhs_scale=g_scales[:],
                start=True,
                stop=True,
            )

        y_sb = keep.tile([P, PACK * N], F32, name="y_sb")
        y_hbm = out_0.rearrange("(p i) n -> p (i n)", i=PACK)

        def step(i, lo, hi, abs_on_vector):
            name = "%d_%d" % (i, lo)
            width = hi - lo
            given = slice((i % 2) * N + lo, (i % 2) * N + hi)
            v = keep.tile([P, width], F32, name="v" + name)
            size = keep.tile([P, width], F32, name="size" + name)
            root = keep.tile([P, width], F32, name="root" + name)
            inverse = keep.tile([P, width], F32, name="inverse" + name)
            soft = keep.tile([P, width], F32, name="soft" + name)
            nc.vector.scalar_tensor_tensor(v[:], accs[i][:, lo:hi], 0.04 / 0.6, mom_sb[i // 2][:, given], ALU.mult, ALU.add)
            if abs_on_vector:
                nc.vector.scalar_tensor_tensor(size[:], v[:], -1.0, v[:], ALU.mult, ALU.max)
            else:
                nc.scalar.activation(size[:], v[:], ACT.Abs)
            nc.scalar.activation(root[:], size[:], ACT.Abs_reciprocal_sqrt, bias=1.0, scale=0.6)
            nc.scalar.activation(inverse[:], root[:], ACT.Square)
            nc.vector.scalar_tensor_tensor(soft[:], v[:], 0.6, inverse[:], ALU.mult, ALU.mult)
            nc.vector.scalar_tensor_tensor(
                y_sb[:, i * N + lo : i * N + hi], old_sb[i // 2][:, given], 0.5, soft[:], ALU.mult, ALU.subtract
            )

        g0 = pick_g(0, 2)
        g0 = weigh_and_round("g_pairs0", g0, rb_spread)
        g1 = pick_g(1, 2)
        g1 = weigh_and_round("g_pairs1", g1, rb_spread)
        turn(g0, g_grouped[:, 0 * P * PACK : 1 * P * PACK], nc.vector.tensor_copy)
        x0 = pick_x(0, "S")
        x0 = weigh_and_round("x_pairs0", x0, ra_spread)
        turn(g1, g_grouped[:, 1 * P * PACK : 2 * P * PACK], nc.vector.tensor_copy)
        x1 = pick_x(1, "S")
        x1 = weigh_and_round("x_pairs1", x1, ra_spread)
        nc.vector.quantize_mx(out=g_codes[:].bitcast(E5M2X4), scales=g_scales[:], in_=g_grouped[:])
        x2 = pick_x(2, "S")
        x2 = weigh_and_round("x_pairs2", x2, ra_spread)
        moment(0, x0, False, nc.scalar.copy)
        x3 = pick_x(3, "S")
        x3 = weigh_and_round("x_pairs3", x3, ra_spread)
        moment(1, x1, False, nc.scalar.copy)
        moment(2, x2, False, nc.scalar.copy)
        moment(3, x3, False, nc.scalar.copy)
        step(0, 0, N // 2, True)
        step(0, N // 2, N, True)
        nc.sync.dma_start(y_hbm[:, 0 * N : 1 * N], y_sb[:, 0 * N : 1 * N])
        step(1, 0, N, True)
        nc.sync.dma_start(y_hbm[:, 1 * N : 2 * N], y_sb[:, 1 * N : 2 * N])
        step(2, 0, N, False)
        nc.sync.dma_start(y_hbm[:, 2 * N : 3 * N], y_sb[:, 2 * N : 3 * N])
        step(3, 0, N // 2, False)
        step(3, N // 2, N, False)
        nc.sync.dma_start(y_hbm[:, 3 * N : 4 * N], y_sb[:, 3 * N : 4 * N])

        y_codes = keep.tile([P, N], U32, name="y_codes", align_bytes=64)
        y_scales = keep.tile([P, N], U8, name="y_scales", align_bytes=64)
        y_planes = y_sb[:].rearrange("p (i n) -> p i n", i=PACK)
        codes_hbm = out_1[0].rearrange("l c r -> l (c r)").bitcast(I32)
        half = N // 2
        y_grouped = [keep.tile([P, half * PACK], BF16, name="y_grouped%d" % c, align_bytes=64) for c in range(2)]
        for c, copy in enumerate((nc.vector.tensor_copy, nc.vector.tensor_copy)):
            cols = slice(c * half, (c + 1) * half)
            copy(y_grouped[c][:].rearrange("p (n i) -> p n i", i=PACK), y_planes[:, :, cols].rearrange("p i n -> p n i"))
        for c in range(2):
            cols = slice(c * half, (c + 1) * half)
            nc.vector.quantize_mx(out=y_codes[:, cols].bitcast(E4M3X4), scales=y_scales[:, cols], in_=y_grouped[c][:])
            nc.sync.dma_start(codes_hbm[:, cols], y_codes[:, cols].bitcast(I32))
        scales_hbm = out_2[0].bitcast(I32)
        for quad in range(4):
            queue = nc.sync if quad < 2 else nc.scalar
            queue.dma_start(scales_hbm[4 * quad : 4 * quad + 4, :], y_scales[32 * quad : 32 * quad + 4, :].bitcast(I32))
